import numpy as np
import ml_dtypes


def mxq(x, axis, fmt="e4m3"):
    dtype, down = {"e4m3": (ml_dtypes.float8_e4m3fn, 7), "e5m2": (ml_dtypes.float8_e5m2, 14)}[fmt]
    v = np.moveaxis(np.asarray(x, np.float32).astype(ml_dtypes.bfloat16).astype(np.float64), axis, -1)
    blocks = v.reshape(v.shape[:-1] + (-1, 32))
    amax = np.abs(blocks).max(-1, keepdims=True)
    byte = np.maximum(np.where(amax > 0, np.frexp(amax)[1] - 1 + 127, 0) - down, 1)
    scale = np.exp2(byte - 127.0)
    codes = (blocks / scale).astype(np.float32).astype(dtype).astype(np.float64)
    return np.moveaxis((codes * scale).reshape(v.shape), -1, axis)


WIDE = False


def mx_kscale(k):
    if not WIDE:
        return np.ones(k)
    levels = np.array([30, -30])
    if k % 512:
        return np.exp2(np.random.permutation(np.resize(levels, k // 32))).repeat(32)
    a = np.empty((k // 512, 16))
    for p in range(k // 512):
        a[p, :8] = np.random.permutation(np.resize(levels, 8))
        for g in range(8):
            far = levels[np.abs(levels - a[p, g]) >= 10]
            a[p, g + 8] = far[np.random.randint(len(far))]
    return np.exp2(a.ravel()).repeat(32)


def f64(x):
    return np.asarray(x).astype(np.float64)


E2M1 = np.array([0.0, 0.5, 1.0, 1.5, 2.0, 3.0, 4.0, 6.0, -0.0, -0.5, -1.0, -1.5, -2.0, -3.0, -4.0, -6.0])


def pack_weight(w, fmt):
    k, n = w.shape
    w = f64(np.asarray(w, np.float32).astype(ml_dtypes.bfloat16)).reshape(k // 32, 32, n)
    amax = np.abs(w).max(1)
    if fmt == "e4m3":
        byte = np.frexp(amax)[1] - 1 + 127 - 7
    else:
        mant, ex = np.frexp(amax / 6.0)
        byte = np.where(mant > 0.5, ex, ex - 1) + 127
    byte = np.clip(np.where(amax > 0, byte, 1), 1, 254)
    scaled = (w * np.exp2(127.0 - byte)[:, None, :]).reshape(k, n).astype(np.float32)
    by_word = np.ascontiguousarray(scaled.reshape(k // 512, 128, 4, n).transpose(0, 1, 3, 2))
    if fmt == "e4m3":
        words = by_word.astype(ml_dtypes.float8_e4m3fn).view(np.uint8)
    else:
        c = by_word.astype(ml_dtypes.float4_e2m1fn).view(np.uint8) & 0xF
        words = (c[..., 0::2] | (c[..., 1::2] << 4)).reshape(k // 512, 128, 2 * n)
    return np.ascontiguousarray(words), np.ascontiguousarray(byte.astype(np.uint8).reshape(k // 512, 16, n))


def unpack_weight(words, scales, fmt):
    g, _, n = scales.shape
    words = np.ascontiguousarray(words).reshape(g, 128, n, -1)
    if fmt == "e4m3":
        vals = words.view(ml_dtypes.float8_e4m3fn).astype(np.float64)
    else:
        nib = np.empty((g, 128, n, 4), np.uint8)
        nib[..., 0::2] = words & 0xF
        nib[..., 1::2] = words >> 4
        vals = E2M1[nib]
    vals = vals * np.repeat(np.exp2(scales.astype(np.float64) - 127.0), 8, axis=1)[..., None]
    return vals.transpose(0, 1, 3, 2).reshape(g * 512, n)


O, T, D, H = 512, 1536, 512, 1024


def setup_inputs():
    n = np.random.standard_normal
    s = mx_kscale(T)[:, None]
    m = np.exp(0.5 * n((T, 1)))
    x = n((T, D)) * s
    p_x4 = pack_weight(x[:O], "e2m1")
    return {
        "x4_words": p_x4[0],
        "x4_scales": p_x4[1],
        "x8": (x[O:]).astype(np.float32),
        "dy": (m * n((T, H)) / np.sqrt(T) / s).astype(np.float32),
    }


def reference(x4_words, x4_scales, x8, dy):
    x4_ = unpack_weight(x4_words, x4_scales, "e2m1")
    x8_ = mxq(f64(x8), 0, "e4m3")
    dy_ = mxq(f64(dy), 0, "e5m2")
    y = x4_.T @ dy_[:O] + x8_.T @ dy_[O:]
    return y

@@ -1,0 +1,135 @@
+from contextlib import ExitStack
+
+import concourse.mybir as mybir
+
+F32 = mybir.dt.float32
+BF16 = mybir.dt.bfloat16
+I32 = mybir.dt.int32
+U32 = mybir.dt.uint32
+U8 = mybir.dt.uint8
+E4M3X4 = mybir.dt.float8_e4m3fn_x4
+E5M2X4 = mybir.dt.float8_e5m2_x4
+E2M1X4 = mybir.dt.float4_e2m1fn_x4
+
+T, D, H = 1536, 512, 1024
+P = 128
+PACK = 4
+K_PASS = P * PACK
+M_TILE = 128
+N_TILE = 512
+M_TILES = D // M_TILE
+V_COLS = 320
+
+FLOPS = 2 * T * D * H
+
+
+def tile_mix_dwsav_none_kernel(tc, x4_words, x4_scales, x8, dy, out):
+    nc = tc.nc
+    with ExitStack() as ctx:
+        keep = ctx.enter_context(tc.tile_pool(name="keep", bufs=1))
+        psum = ctx.enter_context(tc.psum_pool(name="psum", bufs=1))
+        ctx.enter_context(tc.manual_schedule())
+
+        x4_codes = keep.tile([P, 2 * D], U8, name="x4_codes", align_bytes=64)
+        x4_plane = keep.tile([P, D], U8, name="x4_plane", align_bytes=64)
+        nc.vector.memset(x4_plane[:].bitcast(I32), 0)
+
+        def load(name, rows, width):
+            raw = keep.tile([P, PACK, width], F32, name="raw_" + name, align_bytes=64)
+            nc.sync.dma_start(out=raw[:], in_=rows.rearrange("(p j) w -> p j w", j=PACK))
+            return raw
+
+        def interleave(engine_copy, raw, grouped, c0, c1):
+            src = raw[:, :, c0:c1].rearrange("p j (c i) -> p c j i", i=4)
+            dst = grouped[:, 4 * c0 : 4 * c1].rearrange("p (c i j) -> p c j i", i=4, j=PACK)
+            engine_copy(out=dst, in_=src)
+
+        def quantize(name, raw, width, fmt, pieces):
+            grouped = keep.tile([P, PACK * width], BF16, name="grp_" + name, align_bytes=64)
+            codes = keep.tile([P, width], U32, name="codes_" + name, align_bytes=64)
+            plane = keep.tile([P, width], U8, name="plane_" + name, align_bytes=64)
+            c0 = 0
+            for piece in pieces:
+                cv = c0 + (piece * V_COLS) // N_TILE
+                interleave(nc.vector.tensor_copy, raw, grouped, c0, cv)
+                interleave(nc.scalar.copy, raw, grouped, cv, c0 + piece)
+                nc.vector.quantize_mx(
+                    out=codes[:, c0 : c0 + piece].bitcast(fmt),
+                    scales=plane[:, c0 : c0 + piece],
+                    in_=grouped[:, 4 * c0 : 4 * (c0 + piece)],
+                )
+                c0 += piece
+            return codes, plane
+
+        def dy_rows(a, n):
+            return dy[a * K_PASS : (a + 1) * K_PASS, n * N_TILE : (n + 1) * N_TILE]
+
+        nc.sync.dma_start(out=x4_codes[:].bitcast(I32), in_=x4_words[0].bitcast(I32))
+        dy_raw = {}
+        x8_raw = {}
+        dy_raw[0, 0] = load("dy00", dy_rows(0, 0), N_TILE)
+        for q in range(4):
+            nc.sync.dma_start(
+                out=x4_plane[32 * q : 32 * q + 4, :].bitcast(I32),
+                in_=x4_scales[0, 4 * q : 4 * q + 4, :].bitcast(I32),
+            )
+        x8_raw[1] = load("x81", x8[0:K_PASS, :], D)
+        dy_raw[1, 0] = load("dy10", dy_rows(1, 0), N_TILE)
+        x8_raw[2] = load("x82", x8[K_PASS : 2 * K_PASS, :], D)
+        dy_raw[2, 0] = load("dy20", dy_rows(2, 0), N_TILE)
+        dy_raw[0, 1] = load("dy01", dy_rows(0, 1), N_TILE)
+        dy_raw[1, 1] = load("dy11", dy_rows(1, 1), N_TILE)
+        last = keep.tile([P, PACK, N_TILE], F32, name="raw_dy21", align_bytes=64)
+        rows = dy_rows(2, 1).rearrange("(p j) w -> p j w", j=PACK)
+        half = N_TILE // 2
+        nc.sync.dma_start(out=last[:, :, 0:half], in_=rows[:, :, 0:half])
+        nc.sync.dma_start(out=last[:, :, half:], in_=rows[:, :, half:])
+        dy_raw[2, 1] = last
+
+        acc = {}
+        for n in range(2):
+            for m in range(M_TILES):
+                acc[m, n] = psum.tile([M_TILE, N_TILE], F32, name="acc_%d%d" % (m, n))
+        stat = {}
+
+        def multiply(a, n, moving):
+            codes, plane = moving
+            for m in range(M_TILES):
+                cols = slice(m * M_TILE, (m + 1) * M_TILE)
+                if a == 0:
+                    lhsT = x4_codes[:, 2 * m * M_TILE : 2 * (m + 1) * M_TILE].bitcast(E2M1X4)
+                    lhsT_scale = x4_plane[:, cols]
+                else:
+                    lhsT = stat[a][0][:, cols].bitcast(E4M3X4)
+                    lhsT_scale = stat[a][1][:, cols]
+                nc.tensor.matmul_mx(
+                    out=acc[m, n][:],
+                    lhsT=lhsT,
+                    lhsT_scale=lhsT_scale,
+                    rhs=codes[:].bitcast(E5M2X4),
+                    rhs_scale=plane[:],
+                    start=(a == 0),
+                    stop=(a == 2),
+                )
+
+        results = keep.tile([P, M_TILES, N_TILE], F32, name="results0", align_bytes=64)
+        full = [N_TILE]
+        multiply(0, 0, quantize("dy00", dy_raw[0, 0], N_TILE, E5M2X4, full))
+        stat[1] = quantize("x81", x8_raw[1], D, E4M3X4, full)
+        multiply(1, 0, quantize("dy10", dy_raw[1, 0], N_TILE, E5M2X4, full))
+        stat[2] = quantize("x82", x8_raw[2], D, E4M3X4, full)
+        multiply(2, 0, quantize("dy20", dy_raw[2, 0], N_TILE, E5M2X4, full))
+        multiply(0, 1, quantize("dy01", dy_raw[0, 1], N_TILE, E5M2X4, full))
+        for m in range(M_TILES):
+            copy = nc.vector.tensor_copy if m % 2 == 0 else nc.scalar.copy
+            copy(out=results[:, m, :], in_=acc[m, 0][:])
+        nc.sync.dma_start(
+            out=out[:, 0:N_TILE].rearrange("(m p) h -> p m h", p=P), in_=results[:]
+        )
+        multiply(1, 1, quantize("dy11", dy_raw[1, 1], N_TILE, E5M2X4, full))
+        multiply(2, 1, quantize("dy21", dy_raw[2, 1], N_TILE, E5M2X4, [half, half]))
+        for m in range(M_TILES):
+            res = keep.tile([M_TILE, N_TILE], F32, name="res1_%d" % m, align_bytes=64)
+            copy = nc.vector.tensor_copy if m % 2 == 0 else nc.scalar.copy
+            copy(out=res[:], in_=acc[m, 1][:])
+            nc.sync.dma_start(out=out[m * M_TILE : (m + 1) * M_TILE, N_TILE:], in_=res[:])

@@ -65,26 +65,26 @@ def tile_mix_dwsav_none_kernel(tc, x4_words, x4_scales, x8, dy, out):
             return dy[a * K_PASS : (a + 1) * K_PASS, n * N_TILE : (n + 1) * N_TILE]
 
         nc.sync.dma_start(out=x4_codes[:].bitcast(I32), in_=x4_words[0].bitcast(I32))
-        dy_raw = {}
-        x8_raw = {}
-        dy_raw[0, 0] = load("dy00", dy_rows(0, 0), N_TILE)
+
+        def dy_pass(a):
+            return dy[a * K_PASS : (a + 1) * K_PASS, :]
+
+        dy_raw = [load("dy0", dy_pass(0), H)]
         for q in range(4):
             nc.sync.dma_start(
                 out=x4_plane[32 * q : 32 * q + 4, :].bitcast(I32),
                 in_=x4_scales[0, 4 * q : 4 * q + 4, :].bitcast(I32),
             )
+        x8_raw = {}
         x8_raw[1] = load("x81", x8[0:K_PASS, :], D)
-        dy_raw[1, 0] = load("dy10", dy_rows(1, 0), N_TILE)
         x8_raw[2] = load("x82", x8[K_PASS : 2 * K_PASS, :], D)
-        dy_raw[2, 0] = load("dy20", dy_rows(2, 0), N_TILE)
-        dy_raw[0, 1] = load("dy01", dy_rows(0, 1), N_TILE)
-        dy_raw[1, 1] = load("dy11", dy_rows(1, 1), N_TILE)
-        last = keep.tile([P, PACK, N_TILE], F32, name="raw_dy21", align_bytes=64)
-        rows = dy_rows(2, 1).rearrange("(p j) w -> p j w", j=PACK)
+        dy_raw.append(load("dy1", dy_pass(1), H))
+        last = keep.tile([P, PACK, H], F32, name="raw_dy2", align_bytes=64)
+        rows = dy_pass(2).rearrange("(p j) w -> p j w", j=PACK)
         half = N_TILE // 2
-        nc.sync.dma_start(out=last[:, :, 0:half], in_=rows[:, :, 0:half])
-        nc.sync.dma_start(out=last[:, :, half:], in_=rows[:, :, half:])
-        dy_raw[2, 1] = last
+        for lo, hi in ((0, 512), (512, 768), (768, 1024)):
+            nc.sync.dma_start(out=last[:, :, lo:hi], in_=rows[:, :, lo:hi])
+        dy_raw.append(last)
 
         acc = {}
         for n in range(2):
@@ -112,24 +112,30 @@ def tile_mix_dwsav_none_kernel(tc, x4_words, x4_scales, x8, dy, out):
                     stop=(a == 2),
                 )
 
-        results = keep.tile([P, M_TILES, N_TILE], F32, name="results0", align_bytes=64)
         full = [N_TILE]
-        multiply(0, 0, quantize("dy00", dy_raw[0, 0], N_TILE, E5M2X4, full))
+
+        def dy_half(a, n, pieces):
+            raw = dy_raw[a][:, :, n * N_TILE : (n + 1) * N_TILE]
+            return quantize("dy%d%d" % (a, n), raw, N_TILE, E5M2X4, pieces)
+
+        def drain(m, n):
+            res = keep.tile([M_TILE, N_TILE], F32, name="res%d_%d" % (n, m), align_bytes=64)
+            copy = nc.vector.tensor_copy if m % 2 == 0 else nc.scalar.copy
+            copy(out=res[:], in_=acc[m, n][:])
+            nc.sync.dma_start(
+                out=out[m * M_TILE : (m + 1) * M_TILE, n * N_TILE : (n + 1) * N_TILE], in_=res[:]
+            )
+
+        multiply(0, 0, dy_half(0, 0, full))
+        multiply(0, 1, dy_half(0, 1, full))
         stat[1] = quantize("x81", x8_raw[1], D, E4M3X4, full)
-        multiply(1, 0, quantize("dy10", dy_raw[1, 0], N_TILE, E5M2X4, full))
         stat[2] = quantize("x82", x8_raw[2], D, E4M3X4, full)
-        multiply(2, 0, quantize("dy20", dy_raw[2, 0], N_TILE, E5M2X4, full))
-        multiply(0, 1, quantize("dy01", dy_raw[0, 1], N_TILE, E5M2X4, full))
+        multiply(1, 0, dy_half(1, 0, full))
+        multiply(1, 1, dy_half(1, 1, full))
+        multiply(2, 0, dy_half(2, 0, full))
+        tail = dy_half(2, 1, [half, half])
         for m in range(M_TILES):
-            copy = nc.vector.tensor_copy if m % 2 == 0 else nc.scalar.copy
-            copy(out=results[:, m, :], in_=acc[m, 0][:])
-        nc.sync.dma_start(
-            out=out[:, 0:N_TILE].rearrange("(m p) h -> p m h", p=P), in_=results[:]
-        )
-        multiply(1, 1, quantize("dy11", dy_raw[1, 1], N_TILE, E5M2X4, full))
-        multiply(2, 1, quantize("dy21", dy_raw[2, 1], N_TILE, E5M2X4, [half, half]))
+            drain(m, 0)
+        multiply(2, 1, tail)
         for m in range(M_TILES):
-            res = keep.tile([M_TILE, N_TILE], F32, name="res1_%d" % m, align_bytes=64)
-            copy = nc.vector.tensor_copy if m % 2 == 0 else nc.scalar.copy
-            copy(out=res[:], in_=acc[m, 1][:])
-            nc.sync.dma_start(out=out[m * M_TILE : (m + 1) * M_TILE, N_TILE:], in_=res[:])
+            drain(m, 1)

@@ -18,9 +18,11 @@ K_PASS = P * PACK
 M_TILE = 128
 N_TILE = 512
 M_TILES = D // M_TILE
-V_COLS = 320
 
 FLOPS = 2 * T * D * H
+
+
+HALF = N_TILE // 2
 
 
 def tile_mix_dwsav_none_kernel(tc, x4_words, x4_scales, x8, dy, out):
@@ -34,108 +36,124 @@ def tile_mix_dwsav_none_kernel(tc, x4_words, x4_scales, x8, dy, out):
         x4_plane = keep.tile([P, D], U8, name="x4_plane", align_bytes=64)
         nc.vector.memset(x4_plane[:].bitcast(I32), 0)
 
-        def load(name, rows, width):
-            raw = keep.tile([P, PACK, width], F32, name="raw_" + name, align_bytes=64)
+        def load(name, src, row0, cols):
+            raw = keep.tile([P, PACK, cols.stop - cols.start], F32, name="raw_" + name, align_bytes=64)
+            rows = src[row0 : row0 + K_PASS, cols]
             nc.sync.dma_start(out=raw[:], in_=rows.rearrange("(p j) w -> p j w", j=PACK))
             return raw
 
-        def interleave(engine_copy, raw, grouped, c0, c1):
-            src = raw[:, :, c0:c1].rearrange("p j (c i) -> p c j i", i=4)
-            dst = grouped[:, 4 * c0 : 4 * c1].rearrange("p (c i j) -> p c j i", i=4, j=PACK)
-            engine_copy(out=dst, in_=src)
+        def load_dy(a, lo, hi):
+            return load("dy%d_%d" % (a, lo), dy, a * K_PASS, slice(lo, hi))
 
-        def quantize(name, raw, width, fmt, pieces):
-            grouped = keep.tile([P, PACK * width], BF16, name="grp_" + name, align_bytes=64)
-            codes = keep.tile([P, width], U32, name="codes_" + name, align_bytes=64)
-            plane = keep.tile([P, width], U8, name="plane_" + name, align_bytes=64)
-            c0 = 0
-            for piece in pieces:
-                cv = c0 + (piece * V_COLS) // N_TILE
-                interleave(nc.vector.tensor_copy, raw, grouped, c0, cv)
-                interleave(nc.scalar.copy, raw, grouped, cv, c0 + piece)
-                nc.vector.quantize_mx(
-                    out=codes[:, c0 : c0 + piece].bitcast(fmt),
-                    scales=plane[:, c0 : c0 + piece],
-                    in_=grouped[:, 4 * c0 : 4 * (c0 + piece)],
-                )
-                c0 += piece
-            return codes, plane
+        def load_x8(a):
+            return load("x8_%d" % a, x8, (a - 1) * K_PASS, slice(0, D))
 
-        def dy_rows(a, n):
-            return dy[a * K_PASS : (a + 1) * K_PASS, n * N_TILE : (n + 1) * N_TILE]
-
+        dy00 = load_dy(0, 0, N_TILE)
         nc.sync.dma_start(out=x4_codes[:].bitcast(I32), in_=x4_words[0].bitcast(I32))
-
-        def dy_pass(a):
-            return dy[a * K_PASS : (a + 1) * K_PASS, :]
-
-        dy_raw = [load("dy0", dy_pass(0), H)]
         for q in range(4):
             nc.sync.dma_start(
                 out=x4_plane[32 * q : 32 * q + 4, :].bitcast(I32),
                 in_=x4_scales[0, 4 * q : 4 * q + 4, :].bitcast(I32),
             )
-        x8_raw = {}
-        x8_raw[1] = load("x81", x8[0:K_PASS, :], D)
-        x8_raw[2] = load("x82", x8[K_PASS : 2 * K_PASS, :], D)
-        dy_raw.append(load("dy1", dy_pass(1), H))
-        last = keep.tile([P, PACK, H], F32, name="raw_dy2", align_bytes=64)
-        rows = dy_pass(2).rearrange("(p j) w -> p j w", j=PACK)
-        half = N_TILE // 2
-        for lo, hi in ((0, 512), (512, 768), (768, 1024)):
-            nc.sync.dma_start(out=last[:, :, lo:hi], in_=rows[:, :, lo:hi])
-        dy_raw.append(last)
+        x81 = load_x8(1)
+        dy10 = load_dy(1, 0, N_TILE)
+        x82 = load_x8(2)
+        dy20 = load_dy(2, 0, N_TILE)
+        dy01 = load_dy(0, N_TILE, H)
+        dy11 = load_dy(1, N_TILE, H)
+        dy21a = load_dy(2, N_TILE, H - 128)
+        dy21b = load_dy(2, H - 128, H)
 
         acc = {}
         for n in range(2):
             for m in range(M_TILES):
                 acc[m, n] = psum.tile([M_TILE, N_TILE], F32, name="acc_%d%d" % (m, n))
-        stat = {}
 
-        def multiply(a, n, moving):
-            codes, plane = moving
+        def operand(name):
+            grouped = keep.tile([P, PACK * N_TILE], BF16, name="grouped_" + name, align_bytes=64)
+            codes = keep.tile([P, N_TILE], U32, name="codes_" + name, align_bytes=64)
+            plane = keep.tile([P, N_TILE], U8, name="plane_" + name, align_bytes=64)
+            return grouped, codes, plane
+
+        def interleave(copy, raw, lo, op, at, width):
+            copy(
+                out=op[0][:, PACK * at : PACK * (at + width)].rearrange("p (c i j) -> p c j i", i=4, j=PACK),
+                in_=raw[:, :, lo : lo + width].rearrange("p j (c i) -> p c j i", i=4),
+            )
+
+        def quantize(op, fmt, at, width):
+            nc.vector.quantize_mx(
+                out=op[1][:, at : at + width].bitcast(fmt),
+                scales=op[2][:, at : at + width],
+                in_=op[0][:, PACK * at : PACK * (at + width)],
+            )
+
+        def whole(name, raw, fmt, v_cols):
+            op = operand(name)
+            interleave(nc.vector.tensor_copy, raw, 0, op, 0, v_cols)
+            interleave(nc.scalar.copy, raw, v_cols, op, v_cols, N_TILE - v_cols)
+            quantize(op, fmt, 0, N_TILE)
+            return op
+
+        def in_halves(name, raw, fmt):
+            op = operand(name)
+            interleave(nc.vector.tensor_copy, raw, 0, op, 0, HALF)
+            interleave(nc.scalar.copy, raw, HALF, op, HALF, HALF)
+            quantize(op, fmt, 0, HALF)
+            quantize(op, fmt, HALF, HALF)
+            return op
+
+        def multiply(a, n, stationary, moving):
             for m in range(M_TILES):
                 cols = slice(m * M_TILE, (m + 1) * M_TILE)
                 if a == 0:
                     lhsT = x4_codes[:, 2 * m * M_TILE : 2 * (m + 1) * M_TILE].bitcast(E2M1X4)
                     lhsT_scale = x4_plane[:, cols]
                 else:
-                    lhsT = stat[a][0][:, cols].bitcast(E4M3X4)
-                    lhsT_scale = stat[a][1][:, cols]
+                    lhsT = stationary[1][:, cols].bitcast(E4M3X4)
+                    lhsT_scale = stationary[2][:, cols]
                 nc.tensor.matmul_mx(
                     out=acc[m, n][:],
                     lhsT=lhsT,
                     lhsT_scale=lhsT_scale,
-                    rhs=codes[:].bitcast(E5M2X4),
-                    rhs_scale=plane[:],
+                    rhs=moving[1][:].bitcast(E5M2X4),
+                    rhs_scale=moving[2][:],
                     start=(a == 0),
                     stop=(a == 2),
                 )
 
-        full = [N_TILE]
-
-        def dy_half(a, n, pieces):
-            raw = dy_raw[a][:, :, n * N_TILE : (n + 1) * N_TILE]
-            return quantize("dy%d%d" % (a, n), raw, N_TILE, E5M2X4, pieces)
-
-        def drain(m, n):
-            res = keep.tile([M_TILE, N_TILE], F32, name="res%d_%d" % (n, m), align_bytes=64)
+        multiply(0, 0, None, whole("dy00", dy00, E5M2X4, 288))
+        s1 = whole("x81", x81, E4M3X4, 288)
+        multiply(1, 0, s1, whole("dy10", dy10, E5M2X4, 288))
+        s2 = whole("x82", x82, E4M3X4, 288)
+        multiply(2, 0, s2, whole("dy20", dy20, E5M2X4, 288))
+        multiply(0, 1, None, whole("dy01", dy01, E5M2X4, 352))
+        op11 = in_halves("dy11", dy11, E5M2X4)
+        multiply(1, 1, s1, op11)
+        left = keep.tile([M_TILE, M_TILES, N_TILE], F32, name="left", align_bytes=64)
+        for m in range(M_TILES):
             copy = nc.vector.tensor_copy if m % 2 == 0 else nc.scalar.copy
-            copy(out=res[:], in_=acc[m, n][:])
-            nc.sync.dma_start(
-                out=out[m * M_TILE : (m + 1) * M_TILE, n * N_TILE : (n + 1) * N_TILE], in_=res[:]
-            )
+            copy(out=left[:, m, :], in_=acc[m, 0][:])
+        nc.sync.dma_start(out=out[:, 0:N_TILE].rearrange("(m p) h -> p m h", p=M_TILE), in_=left[:])
 
-        multiply(0, 0, dy_half(0, 0, full))
-        multiply(0, 1, dy_half(0, 1, full))
-        stat[1] = quantize("x81", x8_raw[1], D, E4M3X4, full)
-        stat[2] = quantize("x82", x8_raw[2], D, E4M3X4, full)
-        multiply(1, 0, dy_half(1, 0, full))
-        multiply(1, 1, dy_half(1, 1, full))
-        multiply(2, 0, dy_half(2, 0, full))
-        tail = dy_half(2, 1, [half, half])
+        op21 = operand("dy21")
+        interleave(nc.vector.tensor_copy, dy21a, 0, op21, 0, 256)
+        interleave(nc.scalar.copy, dy21a, 256, op21, 256, 128)
+        quantize(op21, E5M2X4, 0, 256)
+        quantize(op21, E5M2X4, 256, 128)
+        interleave(nc.scalar.copy, dy21b, 0, op21, 384, 128)
+        quantize(op21, E5M2X4, 384, 128)
+        multiply(2, 1, s2, op21)
         for m in range(M_TILES):
-            drain(m, 0)
-        multiply(2, 1, tail)
-        for m in range(M_TILES):
-            drain(m, 1)
+            right = keep.tile([M_TILE, N_TILE], F32, name="right_%d" % m, align_bytes=64)
+            copy = nc.vector.tensor_copy if m % 2 == 0 else nc.scalar.copy
+            queue = nc.sync
+            parts = 2 if m == 0 else 1
+            width = N_TILE // parts
+            for part in range(parts):
+                cols = slice(part * width, (part + 1) * width)
+                copy(out=right[:, cols], in_=acc[m, 1][:, cols])
+                queue.dma_start(
+                    out=out[m * M_TILE : (m + 1) * M_TILE, N_TILE + cols.start : N_TILE + cols.stop],
+                    in_=right[:, cols],
+                )

@@ -128,14 +128,14 @@ def tile_mix_dwsav_none_kernel(tc, x4_words, x4_scales, x8, dy, out):
         s2 = whole("x82", x82, E4M3X4, 288)
         multiply(2, 0, s2, whole("dy20", dy20, E5M2X4, 288))
         multiply(0, 1, None, whole("dy01", dy01, E5M2X4, 352))
-        op11 = in_halves("dy11", dy11, E5M2X4)
-        multiply(1, 1, s1, op11)
         left = keep.tile([M_TILE, M_TILES, N_TILE], F32, name="left", align_bytes=64)
         for m in range(M_TILES):
             copy = nc.vector.tensor_copy if m % 2 == 0 else nc.scalar.copy
             copy(out=left[:, m, :], in_=acc[m, 0][:])
         nc.sync.dma_start(out=out[:, 0:N_TILE].rearrange("(m p) h -> p m h", p=M_TILE), in_=left[:])
 
+        op11 = in_halves("dy11", dy11, E5M2X4)
+        multiply(1, 1, s1, op11)
         op21 = operand("dy21")
         interleave(nc.vector.tensor_copy, dy21a, 0, op21, 0, 256)
         interleave(nc.scalar.copy, dy21a, 256, op21, 256, 128)

from contextlib import ExitStack

import concourse.mybir as mybir

F32 = mybir.dt.float32
BF16 = mybir.dt.bfloat16
I32 = mybir.dt.int32
U32 = mybir.dt.uint32
U8 = mybir.dt.uint8
E4M3X4 = mybir.dt.float8_e4m3fn_x4
E5M2X4 = mybir.dt.float8_e5m2_x4
E2M1X4 = mybir.dt.float4_e2m1fn_x4

T, D, H = 1536, 512, 1024
P = 128
PACK = 4
K_PASS = P * PACK
M_TILE = 128
N_TILE = 512
M_TILES = D // M_TILE

FLOPS = 2 * T * D * H


HALF = N_TILE // 2


def tile_mix_dwsav_none_kernel(tc, x4_words, x4_scales, x8, dy, out):
    nc = tc.nc
    with ExitStack() as ctx:
        keep = ctx.enter_context(tc.tile_pool(name="keep", bufs=1))
        psum = ctx.enter_context(tc.psum_pool(name="psum", bufs=1))
        ctx.enter_context(tc.manual_schedule())

        x4_codes = keep.tile([P, 2 * D], U8, name="x4_codes", align_bytes=64)
        x4_plane = keep.tile([P, D], U8, name="x4_plane", align_bytes=64)
        nc.vector.memset(x4_plane[:].bitcast(I32), 0)

        def load(name, src, row0, cols):
            raw = keep.tile([P, PACK, cols.stop - cols.start], F32, name="raw_" + name, align_bytes=64)
            rows = src[row0 : row0 + K_PASS, cols]
            nc.sync.dma_start(out=raw[:], in_=rows.rearrange("(p j) w -> p j w", j=PACK))
            return raw

        def load_dy(a, lo, hi):
            return load("dy%d_%d" % (a, lo), dy, a * K_PASS, slice(lo, hi))

        def load_x8(a):
            return load("x8_%d" % a, x8, (a - 1) * K_PASS, slice(0, D))

        dy00 = load_dy(0, 0, N_TILE)
        nc.sync.dma_start(out=x4_codes[:].bitcast(I32), in_=x4_words[0].bitcast(I32))
        for q in range(4):
            nc.sync.dma_start(
                out=x4_plane[32 * q : 32 * q + 4, :].bitcast(I32),
                in_=x4_scales[0, 4 * q : 4 * q + 4, :].bitcast(I32),
            )
        x81 = load_x8(1)
        dy10 = load_dy(1, 0, N_TILE)
        x82 = load_x8(2)
        dy20 = load_dy(2, 0, N_TILE)
        dy01 = load_dy(0, N_TILE, H)
        dy11 = load_dy(1, N_TILE, H)
        dy21a = load_dy(2, N_TILE, H - 128)
        dy21b = load_dy(2, H - 128, H)

        acc = {}
        for n in range(2):
            for m in range(M_TILES):
                acc[m, n] = psum.tile([M_TILE, N_TILE], F32, name="acc_%d%d" % (m, n))

        def operand(name):
            grouped = keep.tile([P, PACK * N_TILE], BF16, name="grouped_" + name, align_bytes=64)
            codes = keep.tile([P, N_TILE], U32, name="codes_" + name, align_bytes=64)
            plane = keep.tile([P, N_TILE], U8, name="plane_" + name, align_bytes=64)
            return grouped, codes, plane

        def interleave(copy, raw, lo, op, at, width):
            copy(
                out=op[0][:, PACK * at : PACK * (at + width)].rearrange("p (c i j) -> p c j i", i=4, j=PACK),
                in_=raw[:, :, lo : lo + width].rearrange("p j (c i) -> p c j i", i=4),
            )

        def quantize(op, fmt, at, width):
            nc.vector.quantize_mx(
                out=op[1][:, at : at + width].bitcast(fmt),
                scales=op[2][:, at : at + width],
                in_=op[0][:, PACK * at : PACK * (at + width)],
            )

        def whole(name, raw, fmt, v_cols):
            op = operand(name)
            interleave(nc.vector.tensor_copy, raw, 0, op, 0, v_cols)
            interleave(nc.scalar.copy, raw, v_cols, op, v_cols, N_TILE - v_cols)
            quantize(op, fmt, 0, N_TILE)
            return op

        def in_halves(name, raw, fmt):
            op = operand(name)
            interleave(nc.vector.tensor_copy, raw, 0, op, 0, HALF)
            interleave(nc.scalar.copy, raw, HALF, op, HALF, HALF)
            quantize(op, fmt, 0, HALF)
            quantize(op, fmt, HALF, HALF)
            return op

        def multiply(a, n, stationary, moving):
            for m in range(M_TILES):
                cols = slice(m * M_TILE, (m + 1) * M_TILE)
                if a == 0:
                    lhsT = x4_codes[:, 2 * m * M_TILE : 2 * (m + 1) * M_TILE].bitcast(E2M1X4)
                    lhsT_scale = x4_plane[:, cols]
                else:
                    lhsT = stationary[1][:, cols].bitcast(E4M3X4)
                    lhsT_scale = stationary[2][:, cols]
                nc.tensor.matmul_mx(
                    out=acc[m, n][:],
                    lhsT=lhsT,
                    lhsT_scale=lhsT_scale,
                    rhs=moving[1][:].bitcast(E5M2X4),
                    rhs_scale=moving[2][:],
                    start=(a == 0),
                    stop=(a == 2),
                )

        multiply(0, 0, None, whole("dy00", dy00, E5M2X4, 288))
        s1 = whole("x81", x81, E4M3X4, 288)
        multiply(1, 0, s1, whole("dy10", dy10, E5M2X4, 288))
        s2 = whole("x82", x82, E4M3X4, 288)
        multiply(2, 0, s2, whole("dy20", dy20, E5M2X4, 288))
        multiply(0, 1, None, whole("dy01", dy01, E5M2X4, 352))
        left = keep.tile([M_TILE, M_TILES, N_TILE], F32, name="left", align_bytes=64)
        for m in range(M_TILES):
            copy = nc.vector.tensor_copy if m % 2 == 0 else nc.scalar.copy
            copy(out=left[:, m, :], in_=acc[m, 0][:])
        nc.sync.dma_start(out=out[:, 0:N_TILE].rearrange("(m p) h -> p m h", p=M_TILE), in_=left[:])

        op11 = in_halves("dy11", dy11, E5M2X4)
        multiply(1, 1, s1, op11)
        op21 = operand("dy21")
        interleave(nc.vector.tensor_copy, dy21a, 0, op21, 0, 256)
        interleave(nc.scalar.copy, dy21a, 256, op21, 256, 128)
        quantize(op21, E5M2X4, 0, 256)
        quantize(op21, E5M2X4, 256, 128)
        interleave(nc.scalar.copy, dy21b, 0, op21, 384, 128)
        quantize(op21, E5M2X4, 384, 128)
        multiply(2, 1, s2, op21)
        for m in range(M_TILES):
            right = keep.tile([M_TILE, N_TILE], F32, name="right_%d" % m, align_bytes=64)
            copy = nc.vector.tensor_copy if m % 2 == 0 else nc.scalar.copy
            queue = nc.sync
            parts = 2 if m == 0 else 1
            width = N_TILE // parts
            for part in range(parts):
                cols = slice(part * width, (part + 1) * width)
                copy(out=right[:, cols], in_=acc[m, 1][:, cols])
                queue.dma_start(
                    out=out[m * M_TILE : (m + 1) * M_TILE, N_TILE + cols.start : N_TILE + cols.stop],
                    in_=right[:, cols],
                )
